import numpy as np
import ml_dtypes


def mxq(x, axis, fmt="e4m3"):
    dtype, down = {"e4m3": (ml_dtypes.float8_e4m3fn, 7), "e5m2": (ml_dtypes.float8_e5m2, 14)}[fmt]
    v = np.moveaxis(np.asarray(x, np.float32).astype(ml_dtypes.bfloat16).astype(np.float64), axis, -1)
    blocks = v.reshape(v.shape[:-1] + (-1, 32))
    amax = np.abs(blocks).max(-1, keepdims=True)
    byte = np.maximum(np.where(amax > 0, np.frexp(amax)[1] - 1 + 127, 0) - down, 1)
    scale = np.exp2(byte - 127.0)
    codes = (blocks / scale).astype(np.float32).astype(dtype).astype(np.float64)
    return np.moveaxis((codes * scale).reshape(v.shape), -1, axis)


WIDE = False


def mx_kscale(k):
    if not WIDE:
        return np.ones(k)
    levels = np.array([10, -10, 5, -5, 0])
    if k % 512:
        return np.exp2(np.random.permutation(np.resize(levels, k // 32))).repeat(32)
    a = np.empty((k // 512, 16))
    for p in range(k // 512):
        a[p, :8] = np.random.permutation(np.resize(levels, 8))
        for g in range(8):
            far = levels[np.abs(levels - a[p, g]) >= 10]
            a[p, g + 8] = far[np.random.randint(len(far))]
    return np.exp2(a.ravel()).repeat(32)


def f64(x):
    return np.asarray(x).astype(np.float64)


def striped8(idx):
    return np.concatenate([x.reshape(-1, 16).T for x in idx]).astype(np.uint16)


def runs(offs, k):
    lists = np.stack([offs[16 * r : 16 * r + 16].T.reshape(-1) for r in range(8)]).astype(np.int64)
    return lists[np.arange(k) % 512 // 64]


def pack_weight(w):
    k, n = w.shape
    w = f64(np.asarray(w, np.float32).astype(ml_dtypes.bfloat16)).reshape(k // 32, 32, n)
    amax = np.abs(w).max(1)
    byte = np.clip(np.where(amax > 0, np.frexp(amax)[1] - 1 + 127 - 7, 1), 1, 254)
    scaled = (w * np.exp2(127.0 - byte)[:, None, :]).reshape(k, n).astype(np.float32)
    words = np.ascontiguousarray(scaled.reshape(k // 512, 128, 4, n).transpose(0, 1, 3, 2)).astype(ml_dtypes.float8_e4m3fn).view(np.uint8)
    return words, np.ascontiguousarray(byte.astype(np.uint8).reshape(k // 512, 16, n))


def unpack_weight(words, scales):
    g, p, n, _ = words.shape
    vals = np.ascontiguousarray(words).view(ml_dtypes.float8_e4m3fn).astype(np.float64) * np.repeat(np.exp2(scales.astype(np.float64) - 127.0), 8, axis=1)[..., None]
    return vals.transpose(0, 1, 3, 2).reshape(g * 512, n)


def sigmoid(v):
    return 1.0 / (1.0 + np.exp(-np.maximum(v, -700.0)))

def planes(y):
    n, m = y.shape
    v = y.astype(np.float32).astype(ml_dtypes.bfloat16).astype(np.float64).reshape(n // 32, 32, m)
    top = np.abs(v).max(1)
    byte = np.clip(np.where(top > 0, np.frexp(top)[1] - 1 + 127 - 7, 1), 1, 254)
    codes = (v * np.exp2(127.0 - byte)[:, None, :]).reshape(n, m).astype(np.float32).astype(ml_dtypes.float8_e4m3fn).view(np.uint8)
    words = codes.reshape(n // 512, 128, 4, m).transpose(0, 1, 3, 2)
    return np.ascontiguousarray(words), np.ascontiguousarray(byte.astype(np.uint8).reshape(n // 512, 16, m))


K, T, S, N, H, W = 512, 2048, 512, 512, 512, 256


def setup_inputs():
    n = np.random.standard_normal
    s = mx_kscale(K)[:, None]
    u = mx_kscale(H)
    packed_xT = pack_weight(n((K, T)) * s)
    packed_w1 = pack_weight(n((K, H)) / np.sqrt(K) / s)
    packed_w2 = pack_weight(n((H, N)) / np.sqrt(H) / u[:, None])
    perm = np.stack([np.random.permutation(S) for _ in range(8)])
    return {
        "x_words": packed_xT[0],
        "x_scales": packed_xT[1],
        "w1_words": packed_w1[0],
        "w1_scales": packed_w1[1],
        "gn": (np.random.uniform(0.5, 1.5, (H, 1)) * u[:, None]).astype(np.float32),
        "w2_words": packed_w2[0],
        "w2_scales": packed_w2[1],
        "offs": striped8(np.random.randint(0, T, (8, S))),
        "n1": striped8(np.stack([np.random.permutation(S) for _ in range(8)])),
        "n2": striped8(np.stack([np.random.permutation(S) for _ in range(8)])),
        "n3": striped8(perm[:, :W]),
        "n4": striped8(perm[:, W:]),
    }


def reference(x_words, x_scales, w1_words, w1_scales, gn, w2_words, w2_scales, offs, n1, n2, n3, n4):
    xq = unpack_weight(x_words, x_scales)[np.arange(K)[:, None], runs(offs, K)]
    y = unpack_weight(w1_words, w1_scales).T @ xq
    sm = np.maximum(y, y[np.arange(H)[:, None], runs(n2, H)])
    ds = np.zeros((H, S))
    ds[np.arange(H)[:, None], runs(n1, H)] = sm
    z = f64(gn) * (ds * sigmoid(y))
    h = unpack_weight(w2_words, w2_scales).T @ mxq(z, 0, "e4m3")
    pb = h[np.arange(N)[:, None], runs(n4, N)]
    pa = h[np.arange(N)[:, None], runs(n3, N)]
    rb = pb * sigmoid(pb - pa)
    ra = pa * sigmoid(pa - pb)
    ds2 = np.zeros((N, S))
    ds2[np.arange(N)[:, None], runs(n3, N)] = ra
    out = ds2.copy()
    out[np.arange(N)[:, None], runs(n4, N)] = rb
    return (out,) + planes(out)

@@ -1,0 +1,207 @@
+from contextlib import ExitStack
+
+import concourse.mybir as mybir
+
+F32 = mybir.dt.float32
+BF16 = mybir.dt.bfloat16
+I32 = mybir.dt.int32
+U32 = mybir.dt.uint32
+U16 = mybir.dt.uint16
+U8 = mybir.dt.uint8
+FP8X4 = mybir.dt.float8_e4m3fn_x4
+ALU = mybir.AluOpType
+SIGMOID = mybir.ActivationFunctionType.Sigmoid
+
+P = 128
+PACK = 4
+T = 2048
+S = 512
+HALF = S // 2
+FLOPS = 2 * 2 * 512 * 512 * 512
+
+
+def words_of(dram):
+    return dram[0].rearrange("p n t -> p (n t)").bitcast(I32)
+
+
+def half(h):
+    return slice(h * HALF, (h + 1) * HALF)
+
+
+def deal(engine, dealt, raw, line):
+    engine.tensor_copy(
+        dealt.rearrange("p (t a i) -> p a t i", t=PACK, i=line),
+        raw.rearrange("p (a i t) -> p a t i", t=PACK, i=line),
+    )
+
+
+def tile_picked_hashsendgduel_none_po_kernel(
+    tc, x_words, x_scales, w1_words, w1_scales, gn, w2_words, w2_scales, offs, n1, n2, n3, n4, out_0, out_1, out_2
+):
+    nc = tc.nc
+    with ExitStack() as ctx:
+        keep = ctx.enter_context(tc.tile_pool(name="keep", bufs=1))
+        psum = ctx.enter_context(tc.psum_pool(name="psum", bufs=1))
+
+        def sb(name, shape, dtype):
+            return keep.tile(shape, dtype, name=name, align_bytes=64)
+
+        def bank(t, h):
+            return psum.tile([P, HALF], F32, name=f"bank{t}{h}")
+
+        offs_l = sb("offs_l", [P, S // 16], U16)
+        n1_l = sb("n1_l", [P, S // 16], U16)
+        n2_l = sb("n2_l", [P, S // 16], U16)
+        n3_l = sb("n3_l", [P, HALF // 16], U16)
+        n4_l = sb("n4_l", [P, HALF // 16], U16)
+        x_tab = sb("x_tab", [P, T], I32)
+        x_tab_s = sb("x_tab_s", [P, T], U8)
+        x_got_s = sb("x_got_s", [P, S], U8)
+        x_s = sb("x_s", [P, S], U8)
+        x_w = [sb(f"x_w{h}", [P, HALF], I32) for h in range(2)]
+        w_raw = [sb(f"w_raw{i}", [P, S], I32) for i in range(2)]
+        w_raw_s = [sb(f"w_raw_s{i}", [P, S], U8) for i in range(2)]
+        w = [[sb(f"w{i}{t}", [P, P], I32) for t in range(PACK)] for i in range(2)]
+        warm = sb("warm", [P, 8], F32)
+        w_s = [sb(f"w_s{i}", [P, S], U8) for i in range(2)]
+        gain = sb("gain", [P, PACK], F32)
+
+        nc.vector.memset(x_tab_s[:].bitcast(I32), 0)
+        nc.vector.memset(w_raw_s[0][:].bitcast(I32), 0)
+        nc.vector.memset(x_s[:].bitcast(I32), 0)
+        nc.gpsimd.memset(warm[:, 0:1], 0.0)
+        nc.gpsimd.memset(w_raw_s[1][:].bitcast(I32), 0)
+
+        nc.sync.dma_start(offs_l[:], offs)
+        nc.scalar.dma_start(x_tab_s[0:P:8, :].bitcast(I32), x_scales[0].bitcast(I32))
+        nc.sync.dma_start(x_tab[:], words_of(x_words))
+        nc.sync.dma_start(w_raw[0][:], words_of(w1_words))
+        for j in range(PACK):
+            nc.scalar.dma_start(w_raw_s[0][j:P:32, :].bitcast(I32), w1_scales[0][j:16:4, :].bitcast(I32))
+        nc.scalar.activation(warm[:, 4:5], warm[:, 0:1], SIGMOID)
+        for j in range(PACK):
+            nc.gpsimd.dma_start(w_raw_s[1][j:P:32, :].bitcast(I32), w2_scales[0][j:16:4, :].bitcast(I32))
+        nc.sync.dma_start(n2_l[:], n2)
+        nc.sync.dma_start(n1_l[:], n1)
+        nc.sync.dma_start(w_raw[1][:], words_of(w2_words))
+        nc.sync.dma_start(gain[:], gn.rearrange("(p t) o -> p (t o)", t=PACK))
+        nc.sync.dma_start(n3_l[:], n3)
+        nc.sync.dma_start(n4_l[:], n4)
+
+        nc.vector.tensor_copy(x_got_s[:], x_tab_s[:].indirect(offs_l[:]))
+        for j in range(PACK):
+            nc.scalar.dma_start(x_s[j:P:32, :].bitcast(I32), x_got_s[8 * j : P : 32, :].bitcast(I32))
+        deal(nc.vector, w_s[0][:], w_raw_s[0][:], 16)
+        for h in range(2):
+            nc.vector.tensor_copy(x_w[h][:].bitcast(U32), x_tab[:].bitcast(U32).indirect(offs_l[:, 16 * h : 16 * h + 16]))
+            for t in range(h, 1 + 3 * h):
+                nc.vector.tensor_copy(w[0][t][:], w_raw[0][:, t:S:PACK])
+        for t in range(PACK):
+            nc.gpsimd.tensor_copy(w[1][t][:], w_raw[1][:, t:S:PACK])
+        deal(nc.gpsimd, w_s[1][:], w_raw_s[1][:], 16)
+
+        def product(i, t, h, codes, scales):
+            acc = bank(t, h)
+            rows = slice(t * P, (t + 1) * P)
+            nc.tensor.matmul_mx(
+                acc[:], lhsT=w[i][t][:].bitcast(FP8X4), lhsT_scale=w_s[i][:, rows],
+                rhs=codes.bitcast(FP8X4), rhs_scale=scales, start=True, stop=True,
+            )
+            return acc
+
+        y = [sb(f"y{t}", [P, S], F32) for t in range(PACK)]
+        sig = [sb(f"sig{t}", [P, S], F32) for t in range(PACK)]
+        got = [sb(f"got{t}", [P, S], F32) for t in range(PACK)]
+        sm = [sb(f"sm{t}", [P, S], F32) for t in range(PACK)]
+        ds = [sb(f"ds{t}", [P, 2 * S], F32) for t in range(PACK)]
+        z = sb("z", [P, PACK, S], BF16)
+        y_acc = {}
+        for t in range(PACK):
+            for h in range(2):
+                y_acc[t, h] = product(0, t, h, x_w[h][:], x_s[:, half(h)])
+                nc.scalar.copy(y[t][:, half(h)], y_acc[t, h][:])
+        for t in range(PACK):
+            for h in range(2):
+                nc.scalar.activation(sig[t][:, half(h)], y_acc[t, h][:], SIGMOID)
+
+        def fetch_y(t, h):
+            nc.vector.tensor_copy(got[t][:, half(h)], y[t][:].indirect(n2_l[:, 16 * h : 16 * h + 16]))
+
+        def make_z(t, cols):
+            nc.vector.scalar_tensor_tensor(
+                z[:, t, cols], ds[t][:, cols], gain[:, t : t + 1], sig[t][:, cols], ALU.mult, ALU.mult
+            )
+
+        fetch_y(0, 0)
+        for t in range(PACK):
+            fetch_y(t, 1)
+            for h in range(2):
+                nc.vector.tensor_tensor(sm[t][:, half(h)], got[t][:, half(h)], y_acc[t, h][:], ALU.max)
+            if t + 1 < PACK:
+                fetch_y(t + 1, 0)
+            if t >= 2:
+                make_z(t - 2, slice(0, S))
+            nc.vector.tensor_copy(ds[t][:].indirect(n1_l[:]), sm[t][:])
+
+        z_in = [sb(f"z_in{h}", [P, HALF, PACK], BF16) for h in range(2)]
+        z_w = [sb(f"z_w{h}", [P, HALF], I32) for h in range(2)]
+        z_s = [sb(f"z_s{h}", [P, HALF], U8) for h in range(2)]
+
+        def z_pair(u, h):
+            return z_in[h][:, :, 2 * u : 2 * u + 2], z[:, 2 * u : 2 * u + 2, half(h)].rearrange("p t c -> p c t")
+
+        def quantize(codes, scales, grouped):
+            nc.vector.quantize_mx(codes.bitcast(FP8X4), scales, grouped[:].rearrange("p c t -> p (c t)"))
+
+        for h in range(2):
+            nc.scalar.copy(*z_pair(0, h))
+        make_z(2, slice(0, S))
+        make_z(3, half(0))
+        make_z(3, half(1))
+        nc.scalar.copy(*z_pair(1, 0))
+        nc.vector.tensor_copy(*z_pair(1, 1))
+        for h in range(2):
+            quantize(z_w[h][:], z_s[h][:], z_in[h])
+
+        hh = [sb(f"h{t}", [P, S], F32) for t in range(PACK)]
+        for t in range(PACK):
+            for h in range(2):
+                acc = product(1, t, h, z_w[h][:], z_s[h][:])
+                nc.scalar.copy(hh[t][:, half(h)], acc[:])
+
+        pa = sb("pa", [P, PACK, HALF], F32)
+        pb = sb("pb", [P, PACK, HALF], F32)
+        diff = sb("diff", [P, PACK, HALF], F32)
+        sa = sb("sa", [P, PACK, HALF], F32)
+        sbb = sb("sbb", [P, PACK, HALF], F32)
+        res = [sb(f"res{t}", [P, S], F32) for t in range(PACK)]
+        for u in range(2):
+            pair = slice(2 * u, 2 * u + 2)
+            for t in (2 * u, 2 * u + 1):
+                nc.vector.tensor_copy(pa[:, t, :], hh[t][:].indirect(n3_l[:]))
+                nc.vector.tensor_copy(pb[:, t, :], hh[t][:].indirect(n4_l[:]))
+            nc.vector.tensor_tensor(diff[:, pair, :], pa[:, pair, :], pb[:, pair, :], ALU.subtract)
+            nc.scalar.activation(sa[:, pair, :], diff[:, pair, :], SIGMOID)
+            nc.scalar.activation(sbb[:, pair, :], diff[:, pair, :], SIGMOID, scale=-1.0)
+
+        o_in = [sb(f"o_in{h}", [P, HALF, PACK], BF16) for h in range(2)]
+        o_w = [sb(f"o_w{h}", [P, HALF], I32) for h in range(2)]
+        o_s = sb("o_s", [P, S], U8)
+        out_rows = out_0.rearrange("(p t) n -> p t n", t=PACK)
+        for u in range(2):
+            for t in (2 * u, 2 * u + 1):
+                nc.vector.tensor_tensor(res[t][:].indirect(n3_l[:]), pa[:, t, :], sa[:, t, :], ALU.mult)
+            for t in (2 * u, 2 * u + 1):
+                nc.vector.tensor_tensor(res[t][:].indirect(n4_l[:]), pb[:, t, :], sbb[:, t, :], ALU.mult)
+                nc.sync.dma_start(out_rows[:, t, :], res[t][:])
+                nc.scalar.copy(o_in[0][:, :, t], res[t][:, half(0)])
+                if u == 0:
+                    nc.scalar.copy(o_in[1][:, :, t], res[t][:, half(1)])
+        for t in (2, 3):
+            nc.vector.tensor_copy(o_in[1][:, :, t], res[t][:, half(1)])
+        for h in range(2):
+            quantize(o_w[h][:], o_s[:, half(h)], o_in[h])
+            nc.sync.dma_start(words_of(out_1)[:, half(h)], o_w[h][:])
+        for j in range(PACK):
+            queue = nc.scalar if j % 2 else nc.sync
+            queue.dma_start(out_2[0][j:16:4, :].bitcast(I32), o_s[j:P:32, :].bitcast(I32))

@@ -46,9 +46,6 @@ def tile_picked_hashsendgduel_none_po_kernel(
         def sb(name, shape, dtype):
             return keep.tile(shape, dtype, name=name, align_bytes=64)
 
-        def bank(t, h):
-            return psum.tile([P, HALF], F32, name=f"bank{t}{h}")
-
         offs_l = sb("offs_l", [P, S // 16], U16)
         n1_l = sb("n1_l", [P, S // 16], U16)
         n2_l = sb("n2_l", [P, S // 16], U16)
@@ -59,86 +56,98 @@ def tile_picked_hashsendgduel_none_po_kernel(
         x_got_s = sb("x_got_s", [P, S], U8)
         x_s = sb("x_s", [P, S], U8)
         x_w = [sb(f"x_w{h}", [P, HALF], I32) for h in range(2)]
-        w_raw = [sb(f"w_raw{i}", [P, S], I32) for i in range(2)]
         w_raw_s = [sb(f"w_raw_s{i}", [P, S], U8) for i in range(2)]
         w = [[sb(f"w{i}{t}", [P, P], I32) for t in range(PACK)] for i in range(2)]
         warm = sb("warm", [P, 8], F32)
         w_s = [sb(f"w_s{i}", [P, S], U8) for i in range(2)]
         gain = sb("gain", [P, PACK], F32)
 
-        nc.vector.memset(x_tab_s[:].bitcast(I32), 0)
-        nc.vector.memset(w_raw_s[0][:].bitcast(I32), 0)
+        def load_scales(queue, tile, dram):
+            for q in range(4):
+                rows = dram[0][4 * q : 4 * q + 4, :].bitcast(I32)
+                queue.dma_start(tile[32 * q : 32 * q + 32, :].bitcast(I32), rows.unsqueeze(0).broadcast_to([8, 4, S // 4]))
+
         nc.vector.memset(x_s[:].bitcast(I32), 0)
         nc.gpsimd.memset(warm[:, 0:1], 0.0)
-        nc.gpsimd.memset(w_raw_s[1][:].bitcast(I32), 0)
-
-        nc.sync.dma_start(offs_l[:], offs)
-        nc.scalar.dma_start(x_tab_s[0:P:8, :].bitcast(I32), x_scales[0].bitcast(I32))
-        nc.sync.dma_start(x_tab[:], words_of(x_words))
-        nc.sync.dma_start(w_raw[0][:], words_of(w1_words))
-        for j in range(PACK):
-            nc.scalar.dma_start(w_raw_s[0][j:P:32, :].bitcast(I32), w1_scales[0][j:16:4, :].bitcast(I32))
         nc.scalar.activation(warm[:, 4:5], warm[:, 0:1], SIGMOID)
-        for j in range(PACK):
-            nc.gpsimd.dma_start(w_raw_s[1][j:P:32, :].bitcast(I32), w2_scales[0][j:16:4, :].bitcast(I32))
+
+        nc.sync.dma_start(x_tab_s[:].bitcast(I32), x_scales[0].bitcast(I32).unsqueeze(1).broadcast_to([16, 8, T // 4]))
+        nc.sync.dma_start(offs_l[:], offs)
+        load_scales(nc.sync, w_raw_s[0], w1_scales)
         nc.sync.dma_start(n2_l[:], n2)
+        nc.sync.dma_start(x_tab[:], words_of(x_words))
+        w_raw = sb("w_raw", [P, S], I32)
+        nc.sync.dma_start(w_raw[:], words_of(w1_words))
         nc.sync.dma_start(n1_l[:], n1)
-        nc.sync.dma_start(w_raw[1][:], words_of(w2_words))
-        nc.sync.dma_start(gain[:], gn.rearrange("(p t) o -> p (t o)", t=PACK))
         nc.sync.dma_start(n3_l[:], n3)
         nc.sync.dma_start(n4_l[:], n4)
+        nc.gpsimd.dma_start(gain[:], gn.rearrange("(p t) o -> p (t o)", t=PACK))
+        load_scales(nc.gpsimd, w_raw_s[1], w2_scales)
 
         nc.vector.tensor_copy(x_got_s[:], x_tab_s[:].indirect(offs_l[:]))
-        for j in range(PACK):
+        for j in range(1, PACK):
             nc.scalar.dma_start(x_s[j:P:32, :].bitcast(I32), x_got_s[8 * j : P : 32, :].bitcast(I32))
+        for q in range(4):
+            nc.vector.tensor_copy(x_s[32 * q : 32 * q + 1, :].bitcast(I32), x_got_s[32 * q : 32 * q + 1, :].bitcast(I32))
         deal(nc.vector, w_s[0][:], w_raw_s[0][:], 16)
         for h in range(2):
             nc.vector.tensor_copy(x_w[h][:].bitcast(U32), x_tab[:].bitcast(U32).indirect(offs_l[:, 16 * h : 16 * h + 16]))
             for t in range(h, 1 + 3 * h):
-                nc.vector.tensor_copy(w[0][t][:], w_raw[0][:, t:S:PACK])
+                nc.vector.tensor_copy(w[0][t][:], w_raw[:, t:S:PACK])
+        w_raw = sb("w_raw", [P, S], I32)
+        nc.sync.dma_start(w_raw[:], words_of(w2_words))
         for t in range(PACK):
-            nc.gpsimd.tensor_copy(w[1][t][:], w_raw[1][:, t:S:PACK])
+            nc.gpsimd.tensor_copy(w[1][t][:], w_raw[:, t:S:PACK])
         deal(nc.gpsimd, w_s[1][:], w_raw_s[1][:], 16)
 
-        def product(i, t, h, codes, scales):
-            acc = bank(t, h)
-            rows = slice(t * P, (t + 1) * P)
-            nc.tensor.matmul_mx(
-                acc[:], lhsT=w[i][t][:].bitcast(FP8X4), lhsT_scale=w_s[i][:, rows],
-                rhs=codes.bitcast(FP8X4), rhs_scale=scales, start=True, stop=True,
-            )
-            return acc
+        def parts(t):
+            return [half(0), half(1)] if t == 0 else [slice(0, S)]
 
-        y = [sb(f"y{t}", [P, S], F32) for t in range(PACK)]
-        sig = [sb(f"sig{t}", [P, S], F32) for t in range(PACK)]
+        def product(i, t, codes, scales, names, dest):
+            rows = slice(t * P, (t + 1) * P)
+            accs = []
+            for cols, name in zip(parts(t), names):
+                acc = psum.tile([P, cols.stop - cols.start], F32, name=name)
+                for h in range(cols.start // HALF, cols.stop // HALF):
+                    nc.tensor.matmul_mx(
+                        acc[:, h * HALF - cols.start : (h + 1) * HALF - cols.start],
+                        lhsT=w[i][t][:].bitcast(FP8X4), lhsT_scale=w_s[i][:, rows],
+                        rhs=codes[h][:].bitcast(FP8X4), rhs_scale=scales[h], start=True, stop=True,
+                    )
+                nc.scalar.copy(dest[:, cols], acc[:])
+                accs.append(acc)
+            return accs
+
+        y = [sb(f"y{t}", [P, S if t == 0 else 2 * S], F32) for t in range(PACK)]
+        sig0 = sb("sig0", [P, S], F32)
+        sig = [sig0[:]] + [y[t][:, S:] for t in range(1, PACK)]
         got = [sb(f"got{t}", [P, S], F32) for t in range(PACK)]
         sm = [sb(f"sm{t}", [P, S], F32) for t in range(PACK)]
         ds = [sb(f"ds{t}", [P, 2 * S], F32) for t in range(PACK)]
         z = sb("z", [P, PACK, S], BF16)
-        y_acc = {}
-        for t in range(PACK):
-            for h in range(2):
-                y_acc[t, h] = product(0, t, h, x_w[h][:], x_s[:, half(h)])
-                nc.scalar.copy(y[t][:, half(h)], y_acc[t, h][:])
-        for t in range(PACK):
-            for h in range(2):
-                nc.scalar.activation(sig[t][:, half(h)], y_acc[t, h][:], SIGMOID)
+        y_acc = []
+        for t, names in enumerate((["b0", "b1"], ["b2"], ["b3"], ["b4"])):
+            y_acc.append(product(0, t, x_w, [x_s[:, half(0)], x_s[:, half(1)]], names, y[t]))
+            if t > 0:
+                nc.scalar.activation(sig[t], y_acc[t][0][:], SIGMOID)
+        for cols, acc in zip(parts(0), y_acc[0]):
+            nc.scalar.activation(sig[0][:, cols], acc[:], SIGMOID)
 
-        def fetch_y(t, h):
-            nc.vector.tensor_copy(got[t][:, half(h)], y[t][:].indirect(n2_l[:, 16 * h : 16 * h + 16]))
+        def fetch_y(t):
+            for cols in parts(t):
+                nc.vector.tensor_copy(got[t][:, cols], y[t][:].indirect(n2_l[:, cols.start // 16 : cols.stop // 16]))
 
         def make_z(t, cols):
             nc.vector.scalar_tensor_tensor(
                 z[:, t, cols], ds[t][:, cols], gain[:, t : t + 1], sig[t][:, cols], ALU.mult, ALU.mult
             )
 
-        fetch_y(0, 0)
+        fetch_y(0)
         for t in range(PACK):
-            fetch_y(t, 1)
-            for h in range(2):
-                nc.vector.tensor_tensor(sm[t][:, half(h)], got[t][:, half(h)], y_acc[t, h][:], ALU.max)
+            for cols, acc in zip(parts(t), y_acc[t]):
+                nc.vector.tensor_tensor(sm[t][:, cols], got[t][:, cols], acc[:], ALU.max)
             if t + 1 < PACK:
-                fetch_y(t + 1, 0)
+                fetch_y(t + 1)
             if t >= 2:
                 make_z(t - 2, slice(0, S))
             nc.vector.tensor_copy(ds[t][:].indirect(n1_l[:]), sm[t][:])
@@ -164,10 +173,8 @@ def tile_picked_hashsendgduel_none_po_kernel(
             quantize(z_w[h][:], z_s[h][:], z_in[h])
 
         hh = [sb(f"h{t}", [P, S], F32) for t in range(PACK)]
-        for t in range(PACK):
-            for h in range(2):
-                acc = product(1, t, h, z_w[h][:], z_s[h][:])
-                nc.scalar.copy(hh[t][:, half(h)], acc[:])
+        for t, names in enumerate((["b5", "b6"], ["b7"], ["b2"], ["b3"])):
+            product(1, t, z_w, [z_s[0][:], z_s[1][:]], names, hh[t])
 
         pa = sb("pa", [P, PACK, HALF], F32)
         pb = sb("pb", [P, PACK, HALF], F32)

@@ -17,6 +17,7 @@ PACK = 4
 T = 2048
 S = 512
 HALF = S // 2
+LEAD = 8
 FLOPS = 2 * 2 * 512 * 512 * 512
 
 
@@ -26,13 +27,6 @@ def words_of(dram):
 
 def half(h):
     return slice(h * HALF, (h + 1) * HALF)
-
-
-def deal(engine, dealt, raw, line):
-    engine.tensor_copy(
-        dealt.rearrange("p (t a i) -> p a t i", t=PACK, i=line),
-        raw.rearrange("p (a i t) -> p a t i", t=PACK, i=line),
-    )
 
 
 def tile_picked_hashsendgduel_none_po_kernel(
@@ -56,64 +50,66 @@ def tile_picked_hashsendgduel_none_po_kernel(
         x_got_s = sb("x_got_s", [P, S], U8)
         x_s = sb("x_s", [P, S], U8)
         x_w = [sb(f"x_w{h}", [P, HALF], I32) for h in range(2)]
-        w_raw_s = [sb(f"w_raw_s{i}", [P, S], U8) for i in range(2)]
-        w = [[sb(f"w{i}{t}", [P, P], I32) for t in range(PACK)] for i in range(2)]
-        warm = sb("warm", [P, 8], F32)
-        w_s = [sb(f"w_s{i}", [P, S], U8) for i in range(2)]
+        raw_s = sb("raw_s", [P, S], U8)
         gain = sb("gain", [P, PACK], F32)
 
-        def load_scales(queue, tile, dram):
-            for q in range(4):
-                rows = dram[0][4 * q : 4 * q + 4, :].bitcast(I32)
-                queue.dma_start(tile[32 * q : 32 * q + 32, :].bitcast(I32), rows.unsqueeze(0).broadcast_to([8, 4, S // 4]))
+        def load_scales(queues, dram):
+            for j, queue in enumerate(queues):
+                queue.dma_start(raw_s[j:P:32, :].bitcast(I32), dram[0][j:16:4, :].bitcast(I32))
 
+        def deal(raw_w, tiles, names):
+            n = len(tiles)
+            ts = slice(tiles[0], tiles[-1] + 1)
+            words = sb(names[0], [P, n, P], I32)
+            scales = sb(names[1], [P, n, P], U8)
+            nc.vector.tensor_copy(
+                scales[:].rearrange("p t (a i) -> p a t i", i=16),
+                raw_s[:].rearrange("p (a i t) -> p a t i", t=PACK, i=16)[:, :, ts, :],
+            )
+            nc.vector.tensor_copy(
+                words[:].rearrange("p t (a i) -> p a t i", i=4),
+                raw_w[:].rearrange("p (a i t) -> p a t i", t=PACK, i=4)[:, :, ts, :],
+            )
+            return [(words[:, k, :], scales[:, k, :]) for k in range(n)]
+
+        nc.vector.memset(x_tab_s[:].bitcast(I32), 0)
+        nc.vector.memset(raw_s[:].bitcast(I32), 0)
         nc.vector.memset(x_s[:].bitcast(I32), 0)
-        nc.gpsimd.memset(warm[:, 0:1], 0.0)
-        nc.scalar.activation(warm[:, 4:5], warm[:, 0:1], SIGMOID)
 
-        nc.sync.dma_start(x_tab_s[:].bitcast(I32), x_scales[0].bitcast(I32).unsqueeze(1).broadcast_to([16, 8, T // 4]))
-        nc.sync.dma_start(offs_l[:], offs)
-        load_scales(nc.sync, w_raw_s[0], w1_scales)
-        nc.sync.dma_start(n2_l[:], n2)
+        for tile, dram in ((offs_l, offs), (n2_l, n2), (n1_l, n1), (n3_l, n3), (n4_l, n4)):
+            nc.sync.dma_start(tile[:], dram)
+        nc.scalar.dma_start(x_tab_s[0:P:8, :].bitcast(I32), x_scales[0].bitcast(I32))
         nc.sync.dma_start(x_tab[:], words_of(x_words))
-        w_raw = sb("w_raw", [P, S], I32)
-        nc.sync.dma_start(w_raw[:], words_of(w1_words))
-        nc.sync.dma_start(n1_l[:], n1)
-        nc.sync.dma_start(n3_l[:], n3)
-        nc.sync.dma_start(n4_l[:], n4)
+        raw_w1 = sb("raw_w", [P, S], I32)
+        nc.sync.dma_start(raw_w1[:], words_of(w1_words))
+        load_scales((nc.gpsimd, nc.gpsimd, nc.sync, nc.sync), w1_scales)
         nc.gpsimd.dma_start(gain[:], gn.rearrange("(p t) o -> p (t o)", t=PACK))
-        load_scales(nc.gpsimd, w_raw_s[1], w2_scales)
 
         nc.vector.tensor_copy(x_got_s[:], x_tab_s[:].indirect(offs_l[:]))
-        for j in range(1, PACK):
+        for j in range(PACK):
             nc.scalar.dma_start(x_s[j:P:32, :].bitcast(I32), x_got_s[8 * j : P : 32, :].bitcast(I32))
-        for q in range(4):
-            nc.vector.tensor_copy(x_s[32 * q : 32 * q + 1, :].bitcast(I32), x_got_s[32 * q : 32 * q + 1, :].bitcast(I32))
-        deal(nc.vector, w_s[0][:], w_raw_s[0][:], 16)
         for h in range(2):
             nc.vector.tensor_copy(x_w[h][:].bitcast(U32), x_tab[:].bitcast(U32).indirect(offs_l[:, 16 * h : 16 * h + 16]))
-            for t in range(h, 1 + 3 * h):
-                nc.vector.tensor_copy(w[0][t][:], w_raw[:, t:S:PACK])
-        w_raw = sb("w_raw", [P, S], I32)
-        nc.sync.dma_start(w_raw[:], words_of(w2_words))
-        for t in range(PACK):
-            nc.gpsimd.tensor_copy(w[1][t][:], w_raw[:, t:S:PACK])
-        deal(nc.gpsimd, w_s[1][:], w_raw_s[1][:], 16)
+        w1 = deal(raw_w1, [0], ("w1_first", "w1_first_s")) + deal(raw_w1, [1, 2, 3], ("w1_rest", "w1_rest_s"))
+        raw_w2 = sb("raw_w", [P, S], I32)
+        nc.sync.dma_start(raw_w2[:], words_of(w2_words))
+        load_scales([nc.sync] * PACK, w2_scales)
 
         def parts(t):
             return [half(0), half(1)] if t == 0 else [slice(0, S)]
 
-        def product(i, t, codes, scales, names, dest):
-            rows = slice(t * P, (t + 1) * P)
+        def product(w, t, codes, scales, names, dest, lead=None):
             accs = []
             for cols, name in zip(parts(t), names):
                 acc = psum.tile([P, cols.stop - cols.start], F32, name=name)
                 for h in range(cols.start // HALF, cols.stop // HALF):
                     nc.tensor.matmul_mx(
                         acc[:, h * HALF - cols.start : (h + 1) * HALF - cols.start],
-                        lhsT=w[i][t][:].bitcast(FP8X4), lhsT_scale=w_s[i][:, rows],
+                        lhsT=w[t][0].bitcast(FP8X4), lhsT_scale=w[t][1],
                         rhs=codes[h][:].bitcast(FP8X4), rhs_scale=scales[h], start=True, stop=True,
                     )
+                if lead is not None and cols.start == 0:
+                    nc.scalar.activation(lead, acc[:, :LEAD], SIGMOID)
                 nc.scalar.copy(dest[:, cols], acc[:])
                 accs.append(acc)
             return accs
@@ -127,11 +123,11 @@ def tile_picked_hashsendgduel_none_po_kernel(
         z = sb("z", [P, PACK, S], BF16)
         y_acc = []
         for t, names in enumerate((["b0", "b1"], ["b2"], ["b3"], ["b4"])):
-            y_acc.append(product(0, t, x_w, [x_s[:, half(0)], x_s[:, half(1)]], names, y[t]))
+            y_acc.append(product(w1, t, x_w, [x_s[:, half(0)], x_s[:, half(1)]], names, y[t], sig0[:, :LEAD] if t == 0 else None))
             if t > 0:
                 nc.scalar.activation(sig[t], y_acc[t][0][:], SIGMOID)
-        for cols, acc in zip(parts(0), y_acc[0]):
-            nc.scalar.activation(sig[0][:, cols], acc[:], SIGMOID)
+        nc.scalar.activation(sig0[:, LEAD:HALF], y_acc[0][0][:, LEAD:], SIGMOID)
+        nc.scalar.activation(sig0[:, HALF:], y_acc[0][1][:], SIGMOID)
 
         def fetch_y(t):
             for cols in parts(t):
@@ -172,9 +168,10 @@ def tile_picked_hashsendgduel_none_po_kernel(
         for h in range(2):
             quantize(z_w[h][:], z_s[h][:], z_in[h])
 
+        w2 = deal(raw_w2, [0], ("w2_first", "w2_first_s")) + deal(raw_w2, [1, 2, 3], ("z_in1", "z_in0"))
         hh = [sb(f"h{t}", [P, S], F32) for t in range(PACK)]
         for t, names in enumerate((["b5", "b6"], ["b7"], ["b2"], ["b3"])):
-            product(1, t, z_w, [z_s[0][:], z_s[1][:]], names, hh[t])
+            product(w2, t, z_w, [z_s[0][:], z_s[1][:]], names, hh[t])
 
         pa = sb("pa", [P, PACK, HALF], F32)
         pb = sb("pb", [P, PACK, HALF], F32)

@@ -11,6 +11,7 @@ U8 = mybir.dt.uint8
 FP8X4 = mybir.dt.float8_e4m3fn_x4
 ALU = mybir.AluOpType
 SIGMOID = mybir.ActivationFunctionType.Sigmoid
+COPY = mybir.ActivationFunctionType.Copy
 
 P = 128
 PACK = 4
@@ -78,7 +79,7 @@ def tile_picked_hashsendgduel_none_po_kernel(
 
         for tile, dram in ((offs_l, offs), (n2_l, n2), (n1_l, n1), (n3_l, n3), (n4_l, n4)):
             nc.sync.dma_start(tile[:], dram)
-        nc.scalar.dma_start(x_tab_s[0:P:8, :].bitcast(I32), x_scales[0].bitcast(I32))
+        nc.sync.dma_start(x_tab_s[0:P:8, :].bitcast(I32), x_scales[0].bitcast(I32))
         nc.sync.dma_start(x_tab[:], words_of(x_words))
         raw_w1 = sb("raw_w", [P, S], I32)
         nc.sync.dma_start(raw_w1[:], words_of(w1_words))
@@ -87,7 +88,8 @@ def tile_picked_hashsendgduel_none_po_kernel(
 
         nc.vector.tensor_copy(x_got_s[:], x_tab_s[:].indirect(offs_l[:]))
         for j in range(PACK):
-            nc.scalar.dma_start(x_s[j:P:32, :].bitcast(I32), x_got_s[8 * j : P : 32, :].bitcast(I32))
+            queue = nc.scalar if j % 2 else nc.sync
+            queue.dma_start(x_s[j:P:32, :].bitcast(I32), x_got_s[8 * j : P : 32, :].bitcast(I32))
         for h in range(2):
             nc.vector.tensor_copy(x_w[h][:].bitcast(U32), x_tab[:].bitcast(U32).indirect(offs_l[:, 16 * h : 16 * h + 16]))
         w1 = deal(raw_w1, [0], ("w1_first", "w1_first_s")) + deal(raw_w1, [1, 2, 3], ("w1_rest", "w1_rest_s"))
@@ -98,7 +100,7 @@ def tile_picked_hashsendgduel_none_po_kernel(
         def parts(t):
             return [half(0), half(1)] if t == 0 else [slice(0, S)]
 
-        def product(w, t, codes, scales, names, dest, lead=None):
+        def product(w, t, codes, scales, names, dest, copy):
             accs = []
             for cols, name in zip(parts(t), names):
                 acc = psum.tile([P, cols.stop - cols.start], F32, name=name)
@@ -108,9 +110,7 @@ def tile_picked_hashsendgduel_none_po_kernel(
                         lhsT=w[t][0].bitcast(FP8X4), lhsT_scale=w[t][1],
                         rhs=codes[h][:].bitcast(FP8X4), rhs_scale=scales[h], start=True, stop=True,
                     )
-                if lead is not None and cols.start == 0:
-                    nc.scalar.activation(lead, acc[:, :LEAD], SIGMOID)
-                nc.scalar.copy(dest[:, cols], acc[:])
+                copy(dest[:, cols], acc, cols)
                 accs.append(acc)
             return accs
 
@@ -121,17 +121,41 @@ def tile_picked_hashsendgduel_none_po_kernel(
         sm = [sb(f"sm{t}", [P, S], F32) for t in range(PACK)]
         ds = [sb(f"ds{t}", [P, 2 * S], F32) for t in range(PACK)]
         z = sb("z", [P, PACK, S], BF16)
+        gate = [sb(f"gate{t}", [P, S], F32) for t in range(PACK - 1)]
+
+        def plain_copy(dest, acc, cols):
+            nc.scalar.copy(dest, acc[:])
+
+        def first_copy(dest, acc, cols):
+            if cols.start == 0:
+                nc.scalar.activation(sig0[:, :LEAD], acc[:, :LEAD], SIGMOID)
+                nc.scalar.copy(dest, acc[:])
+            else:
+                nc.vector.tensor_copy(dest, acc[:])
+
         y_acc = []
         for t, names in enumerate((["b0", "b1"], ["b2"], ["b3"], ["b4"])):
-            y_acc.append(product(w1, t, x_w, [x_s[:, half(0)], x_s[:, half(1)]], names, y[t], sig0[:, :LEAD] if t == 0 else None))
+            copy = first_copy if t == 0 else plain_copy
+            y_acc.append(product(w1, t, x_w, [x_s[:, half(0)], x_s[:, half(1)]], names, y[t], copy))
             if t > 0:
                 nc.scalar.activation(sig[t], y_acc[t][0][:], SIGMOID)
         nc.scalar.activation(sig0[:, LEAD:HALF], y_acc[0][0][:, LEAD:], SIGMOID)
         nc.scalar.activation(sig0[:, HALF:], y_acc[0][1][:], SIGMOID)
+        for t in range(PACK - 1):
+            nc.scalar.activation(gate[t][:], sig[t], COPY, scale=gain[:, t : t + 1])
 
         def fetch_y(t):
             for cols in parts(t):
                 nc.vector.tensor_copy(got[t][:, cols], y[t][:].indirect(n2_l[:, cols.start // 16 : cols.stop // 16]))
+
+        def larger(t):
+            for cols, acc in zip(parts(t), y_acc[t]):
+                nc.vector.tensor_tensor(sm[t][:, cols], got[t][:, cols], acc[:], ALU.max)
+
+        def send(t):
+            nc.vector.tensor_copy(ds[t][:].indirect(n1_l[:]), sm[t][:])
+            if t < PACK - 1:
+                nc.gpsimd.tensor_tensor(z[:, t, :], ds[t][:, :S], gate[t][:], ALU.mult)
 
         def make_z(t, cols):
             nc.vector.scalar_tensor_tensor(
@@ -139,14 +163,18 @@ def tile_picked_hashsendgduel_none_po_kernel(
             )
 
         fetch_y(0)
-        for t in range(PACK):
-            for cols, acc in zip(parts(t), y_acc[t]):
-                nc.vector.tensor_tensor(sm[t][:, cols], got[t][:, cols], acc[:], ALU.max)
-            if t + 1 < PACK:
-                fetch_y(t + 1)
-            if t >= 2:
-                make_z(t - 2, slice(0, S))
-            nc.vector.tensor_copy(ds[t][:].indirect(n1_l[:]), sm[t][:])
+        larger(0)
+        fetch_y(1)
+        send(0)
+        larger(1)
+        fetch_y(2)
+        send(1)
+        fetch_y(3)
+        larger(2)
+        larger(3)
+        send(2)
+        send(3)
+        w2 = deal(raw_w2, [0], ("sm3", "sm2"))
 
         z_in = [sb(f"z_in{h}", [P, HALF, PACK], BF16) for h in range(2)]
         z_w = [sb(f"z_w{h}", [P, HALF], I32) for h in range(2)]
@@ -160,7 +188,6 @@ def tile_picked_hashsendgduel_none_po_kernel(
 
         for h in range(2):
             nc.scalar.copy(*z_pair(0, h))
-        make_z(2, slice(0, S))
         make_z(3, half(0))
         make_z(3, half(1))
         nc.scalar.copy(*z_pair(1, 0))
@@ -168,35 +195,40 @@ def tile_picked_hashsendgduel_none_po_kernel(
         for h in range(2):
             quantize(z_w[h][:], z_s[h][:], z_in[h])
 
-        w2 = deal(raw_w2, [0], ("w2_first", "w2_first_s")) + deal(raw_w2, [1, 2, 3], ("z_in1", "z_in0"))
+        w2 = w2 + deal(raw_w2, [1, 2, 3], ("z_in1", "z_in0"))
         hh = [sb(f"h{t}", [P, S], F32) for t in range(PACK)]
         for t, names in enumerate((["b5", "b6"], ["b7"], ["b2"], ["b3"])):
-            product(w2, t, z_w, [z_s[0][:], z_s[1][:]], names, hh[t])
+            product(w2, t, z_w, [z_s[0][:], z_s[1][:]], names, hh[t], plain_copy)
 
-        pa = sb("pa", [P, PACK, HALF], F32)
-        pb = sb("pb", [P, PACK, HALF], F32)
-        diff = sb("diff", [P, PACK, HALF], F32)
-        sa = sb("sa", [P, PACK, HALF], F32)
-        sbb = sb("sbb", [P, PACK, HALF], F32)
-        res = [sb(f"res{t}", [P, S], F32) for t in range(PACK)]
-        for u in range(2):
-            pair = slice(2 * u, 2 * u + 2)
-            for t in (2 * u, 2 * u + 1):
-                nc.vector.tensor_copy(pa[:, t, :], hh[t][:].indirect(n3_l[:]))
-                nc.vector.tensor_copy(pb[:, t, :], hh[t][:].indirect(n4_l[:]))
-            nc.vector.tensor_tensor(diff[:, pair, :], pa[:, pair, :], pb[:, pair, :], ALU.subtract)
-            nc.scalar.activation(sa[:, pair, :], diff[:, pair, :], SIGMOID)
-            nc.scalar.activation(sbb[:, pair, :], diff[:, pair, :], SIGMOID, scale=-1.0)
+        pa = [sb(f"pa{t}", [P, HALF], F32) for t in range(PACK)]
+        pb = [sb(f"pb{t}", [P, HALF], F32) for t in range(PACK)]
+        diff = [sb(f"diff{t}", [P, HALF], F32) for t in range(PACK)]
+        sa = [sb(f"sa{t}", [P, HALF], F32) for t in range(PACK)]
+        sbb = [sb(f"sbb{t}", [P, HALF], F32) for t in range(PACK)]
 
+        def gates(engine, t):
+            engine.tensor_tensor(diff[t][:], pa[t][:], pb[t][:], ALU.subtract)
+            nc.scalar.activation(sa[t][:], diff[t][:], SIGMOID)
+            nc.scalar.activation(sbb[t][:], diff[t][:], SIGMOID, scale=-1.0)
+
+        for t in range(PACK):
+            nc.vector.tensor_copy(pa[t][:], hh[t][:].indirect(n3_l[:]))
+            nc.vector.tensor_copy(pb[t][:], hh[t][:].indirect(n4_l[:]))
+            if t < PACK - 1:
+                gates(nc.gpsimd, t)
+
+        res = [sb(f"h{PACK - 1 - t}", [P, S], F32) for t in range(PACK)]
         o_in = [sb(f"o_in{h}", [P, HALF, PACK], BF16) for h in range(2)]
         o_w = [sb(f"o_w{h}", [P, HALF], I32) for h in range(2)]
         o_s = sb("o_s", [P, S], U8)
         out_rows = out_0.rearrange("(p t) n -> p t n", t=PACK)
         for u in range(2):
             for t in (2 * u, 2 * u + 1):
-                nc.vector.tensor_tensor(res[t][:].indirect(n3_l[:]), pa[:, t, :], sa[:, t, :], ALU.mult)
+                nc.vector.tensor_tensor(res[t][:].indirect(n3_l[:]), pa[t][:], sa[t][:], ALU.mult)
+                if t == 0:
+                    gates(nc.vector, PACK - 1)
             for t in (2 * u, 2 * u + 1):
-                nc.vector.tensor_tensor(res[t][:].indirect(n4_l[:]), pb[:, t, :], sbb[:, t, :], ALU.mult)
+                nc.vector.tensor_tensor(res[t][:].indirect(n4_l[:]), pb[t][:], sbb[t][:], ALU.mult)
                 nc.sync.dma_start(out_rows[:, t, :], res[t][:])
                 nc.scalar.copy(o_in[0][:, :, t], res[t][:, half(0)])
                 if u == 0:

from contextlib import ExitStack

import concourse.mybir as mybir

F32 = mybir.dt.float32
BF16 = mybir.dt.bfloat16
I32 = mybir.dt.int32
U32 = mybir.dt.uint32
U16 = mybir.dt.uint16
U8 = mybir.dt.uint8
FP8X4 = mybir.dt.float8_e4m3fn_x4
ALU = mybir.AluOpType
SIGMOID = mybir.ActivationFunctionType.Sigmoid
COPY = mybir.ActivationFunctionType.Copy

P = 128
PACK = 4
T = 2048
S = 512
HALF = S // 2
LEAD = 8
FLOPS = 2 * 2 * 512 * 512 * 512


def words_of(dram):
    return dram[0].rearrange("p n t -> p (n t)").bitcast(I32)


def half(h):
    return slice(h * HALF, (h + 1) * HALF)


def tile_picked_hashsendgduel_none_po_kernel(
    tc, x_words, x_scales, w1_words, w1_scales, gn, w2_words, w2_scales, offs, n1, n2, n3, n4, out_0, out_1, out_2
):
    nc = tc.nc
    with ExitStack() as ctx:
        keep = ctx.enter_context(tc.tile_pool(name="keep", bufs=1))
        psum = ctx.enter_context(tc.psum_pool(name="psum", bufs=1))

        def sb(name, shape, dtype):
            return keep.tile(shape, dtype, name=name, align_bytes=64)

        offs_l = sb("offs_l", [P, S // 16], U16)
        n1_l = sb("n1_l", [P, S // 16], U16)
        n2_l = sb("n2_l", [P, S // 16], U16)
        n3_l = sb("n3_l", [P, HALF // 16], U16)
        n4_l = sb("n4_l", [P, HALF // 16], U16)
        x_tab = sb("x_tab", [P, T], I32)
        x_tab_s = sb("x_tab_s", [P, T], U8)
        x_got_s = sb("x_got_s", [P, S], U8)
        x_s = sb("x_s", [P, S], U8)
        x_w = [sb(f"x_w{h}", [P, HALF], I32) for h in range(2)]
        raw_s = sb("raw_s", [P, S], U8)
        gain = sb("gain", [P, PACK], F32)

        def load_scales(queues, dram):
            for j, queue in enumerate(queues):
                queue.dma_start(raw_s[j:P:32, :].bitcast(I32), dram[0][j:16:4, :].bitcast(I32))

        def deal(raw_w, tiles, names):
            n = len(tiles)
            ts = slice(tiles[0], tiles[-1] + 1)
            words = sb(names[0], [P, n, P], I32)
            scales = sb(names[1], [P, n, P], U8)
            nc.vector.tensor_copy(
                scales[:].rearrange("p t (a i) -> p a t i", i=16),
                raw_s[:].rearrange("p (a i t) -> p a t i", t=PACK, i=16)[:, :, ts, :],
            )
            nc.vector.tensor_copy(
                words[:].rearrange("p t (a i) -> p a t i", i=4),
                raw_w[:].rearrange("p (a i t) -> p a t i", t=PACK, i=4)[:, :, ts, :],
            )
            return [(words[:, k, :], scales[:, k, :]) for k in range(n)]

        nc.vector.memset(x_tab_s[:].bitcast(I32), 0)
        nc.vector.memset(raw_s[:].bitcast(I32), 0)
        nc.vector.memset(x_s[:].bitcast(I32), 0)

        for tile, dram in ((offs_l, offs), (n2_l, n2), (n1_l, n1), (n3_l, n3), (n4_l, n4)):
            nc.sync.dma_start(tile[:], dram)
        nc.sync.dma_start(x_tab_s[0:P:8, :].bitcast(I32), x_scales[0].bitcast(I32))
        nc.sync.dma_start(x_tab[:], words_of(x_words))
        raw_w1 = sb("raw_w", [P, S], I32)
        nc.sync.dma_start(raw_w1[:], words_of(w1_words))
        load_scales((nc.gpsimd, nc.gpsimd, nc.sync, nc.sync), w1_scales)
        nc.gpsimd.dma_start(gain[:], gn.rearrange("(p t) o -> p (t o)", t=PACK))

        nc.vector.tensor_copy(x_got_s[:], x_tab_s[:].indirect(offs_l[:]))
        for j in range(PACK):
            queue = nc.scalar if j % 2 else nc.sync
            queue.dma_start(x_s[j:P:32, :].bitcast(I32), x_got_s[8 * j : P : 32, :].bitcast(I32))
        for h in range(2):
            nc.vector.tensor_copy(x_w[h][:].bitcast(U32), x_tab[:].bitcast(U32).indirect(offs_l[:, 16 * h : 16 * h + 16]))
        w1 = deal(raw_w1, [0], ("w1_first", "w1_first_s")) + deal(raw_w1, [1, 2, 3], ("w1_rest", "w1_rest_s"))
        raw_w2 = sb("raw_w", [P, S], I32)
        nc.sync.dma_start(raw_w2[:], words_of(w2_words))
        load_scales([nc.sync] * PACK, w2_scales)

        def parts(t):
            return [half(0), half(1)] if t == 0 else [slice(0, S)]

        def product(w, t, codes, scales, names, dest, copy):
            accs = []
            for cols, name in zip(parts(t), names):
                acc = psum.tile([P, cols.stop - cols.start], F32, name=name)
                for h in range(cols.start // HALF, cols.stop // HALF):
                    nc.tensor.matmul_mx(
                        acc[:, h * HALF - cols.start : (h + 1) * HALF - cols.start],
                        lhsT=w[t][0].bitcast(FP8X4), lhsT_scale=w[t][1],
                        rhs=codes[h][:].bitcast(FP8X4), rhs_scale=scales[h], start=True, stop=True,
                    )
                copy(dest[:, cols], acc, cols)
                accs.append(acc)
            return accs

        y = [sb(f"y{t}", [P, S if t == 0 else 2 * S], F32) for t in range(PACK)]
        sig0 = sb("sig0", [P, S], F32)
        sig = [sig0[:]] + [y[t][:, S:] for t in range(1, PACK)]
        got = [sb(f"got{t}", [P, S], F32) for t in range(PACK)]
        sm = [sb(f"sm{t}", [P, S], F32) for t in range(PACK)]
        ds = [sb(f"ds{t}", [P, 2 * S], F32) for t in range(PACK)]
        z = sb("z", [P, PACK, S], BF16)
        gate = [sb(f"gate{t}", [P, S], F32) for t in range(PACK - 1)]

        def plain_copy(dest, acc, cols):
            nc.scalar.copy(dest, acc[:])

        def first_copy(dest, acc, cols):
            if cols.start == 0:
                nc.scalar.activation(sig0[:, :LEAD], acc[:, :LEAD], SIGMOID)
                nc.scalar.copy(dest, acc[:])
            else:
                nc.vector.tensor_copy(dest, acc[:])

        y_acc = []
        for t, names in enumerate((["b0", "b1"], ["b2"], ["b3"], ["b4"])):
            copy = first_copy if t == 0 else plain_copy
            y_acc.append(product(w1, t, x_w, [x_s[:, half(0)], x_s[:, half(1)]], names, y[t], copy))
            if t > 0:
                nc.scalar.activation(sig[t], y_acc[t][0][:], SIGMOID)
        nc.scalar.activation(sig0[:, LEAD:HALF], y_acc[0][0][:, LEAD:], SIGMOID)
        nc.scalar.activation(sig0[:, HALF:], y_acc[0][1][:], SIGMOID)
        for t in range(PACK - 1):
            nc.scalar.activation(gate[t][:], sig[t], COPY, scale=gain[:, t : t + 1])

        def fetch_y(t):
            for cols in parts(t):
                nc.vector.tensor_copy(got[t][:, cols], y[t][:].indirect(n2_l[:, cols.start // 16 : cols.stop // 16]))

        def larger(t):
            for cols, acc in zip(parts(t), y_acc[t]):
                nc.vector.tensor_tensor(sm[t][:, cols], got[t][:, cols], acc[:], ALU.max)

        def send(t):
            nc.vector.tensor_copy(ds[t][:].indirect(n1_l[:]), sm[t][:])
            if t < PACK - 1:
                nc.gpsimd.tensor_tensor(z[:, t, :], ds[t][:, :S], gate[t][:], ALU.mult)

        def make_z(t, cols):
            nc.vector.scalar_tensor_tensor(
                z[:, t, cols], ds[t][:, cols], gain[:, t : t + 1], sig[t][:, cols], ALU.mult, ALU.mult
            )

        fetch_y(0)
        larger(0)
        fetch_y(1)
        send(0)
        larger(1)
        fetch_y(2)
        send(1)
        fetch_y(3)
        larger(2)
        larger(3)
        send(2)
        send(3)
        w2 = deal(raw_w2, [0], ("sm3", "sm2"))

        z_in = [sb(f"z_in{h}", [P, HALF, PACK], BF16) for h in range(2)]
        z_w = [sb(f"z_w{h}", [P, HALF], I32) for h in range(2)]
        z_s = [sb(f"z_s{h}", [P, HALF], U8) for h in range(2)]

        def z_pair(u, h):
            return z_in[h][:, :, 2 * u : 2 * u + 2], z[:, 2 * u : 2 * u + 2, half(h)].rearrange("p t c -> p c t")

        def quantize(codes, scales, grouped):
            nc.vector.quantize_mx(codes.bitcast(FP8X4), scales, grouped[:].rearrange("p c t -> p (c t)"))

        for h in range(2):
            nc.scalar.copy(*z_pair(0, h))
        make_z(3, half(0))
        make_z(3, half(1))
        nc.scalar.copy(*z_pair(1, 0))
        nc.vector.tensor_copy(*z_pair(1, 1))
        for h in range(2):
            quantize(z_w[h][:], z_s[h][:], z_in[h])

        w2 = w2 + deal(raw_w2, [1, 2, 3], ("z_in1", "z_in0"))
        hh = [sb(f"h{t}", [P, S], F32) for t in range(PACK)]
        for t, names in enumerate((["b5", "b6"], ["b7"], ["b2"], ["b3"])):
            product(w2, t, z_w, [z_s[0][:], z_s[1][:]], names, hh[t], plain_copy)

        pa = [sb(f"pa{t}", [P, HALF], F32) for t in range(PACK)]
        pb = [sb(f"pb{t}", [P, HALF], F32) for t in range(PACK)]
        diff = [sb(f"diff{t}", [P, HALF], F32) for t in range(PACK)]
        sa = [sb(f"sa{t}", [P, HALF], F32) for t in range(PACK)]
        sbb = [sb(f"sbb{t}", [P, HALF], F32) for t in range(PACK)]

        def gates(engine, t):
            engine.tensor_tensor(diff[t][:], pa[t][:], pb[t][:], ALU.subtract)
            nc.scalar.activation(sa[t][:], diff[t][:], SIGMOID)
            nc.scalar.activation(sbb[t][:], diff[t][:], SIGMOID, scale=-1.0)

        for t in range(PACK):
            nc.vector.tensor_copy(pa[t][:], hh[t][:].indirect(n3_l[:]))
            nc.vector.tensor_copy(pb[t][:], hh[t][:].indirect(n4_l[:]))
            if t < PACK - 1:
                gates(nc.gpsimd, t)

        res = [sb(f"h{PACK - 1 - t}", [P, S], F32) for t in range(PACK)]
        o_in = [sb(f"o_in{h}", [P, HALF, PACK], BF16) for h in range(2)]
        o_w = [sb(f"o_w{h}", [P, HALF], I32) for h in range(2)]
        o_s = sb("o_s", [P, S], U8)
        out_rows = out_0.rearrange("(p t) n -> p t n", t=PACK)
        for u in range(2):
            for t in (2 * u, 2 * u + 1):
                nc.vector.tensor_tensor(res[t][:].indirect(n3_l[:]), pa[t][:], sa[t][:], ALU.mult)
                if t == 0:
                    gates(nc.vector, PACK - 1)
            for t in (2 * u, 2 * u + 1):
                nc.vector.tensor_tensor(res[t][:].indirect(n4_l[:]), pb[t][:], sbb[t][:], ALU.mult)
                nc.sync.dma_start(out_rows[:, t, :], res[t][:])
                nc.scalar.copy(o_in[0][:, :, t], res[t][:, half(0)])
                if u == 0:
                    nc.scalar.copy(o_in[1][:, :, t], res[t][:, half(1)])
        for t in (2, 3):
            nc.vector.tensor_copy(o_in[1][:, :, t], res[t][:, half(1)])
        for h in range(2):
            quantize(o_w[h][:], o_s[:, half(h)], o_in[h])
            nc.sync.dma_start(words_of(out_1)[:, half(h)], o_w[h][:])
        for j in range(PACK):
            queue = nc.scalar if j % 2 else nc.sync
            queue.dma_start(out_2[0][j:16:4, :].bitcast(I32), o_s[j:P:32, :].bitcast(I32))
